import numpy as np
import ml_dtypes


def mxq(x, axis, fmt="e4m3"):
    dtype, down = {"e4m3": (ml_dtypes.float8_e4m3fn, 7), "e5m2": (ml_dtypes.float8_e5m2, 14)}[fmt]
    v = np.moveaxis(np.asarray(x, np.float32).astype(ml_dtypes.bfloat16).astype(np.float64), axis, -1)
    blocks = v.reshape(v.shape[:-1] + (-1, 32))
    amax = np.abs(blocks).max(-1, keepdims=True)
    byte = np.maximum(np.where(amax > 0, np.frexp(amax)[1] - 1 + 127, 0) - down, 1)
    scale = np.exp2(byte - 127.0)
    codes = (blocks / scale).astype(np.float32).astype(dtype).astype(np.float64)
    return np.moveaxis((codes * scale).reshape(v.shape), -1, axis)


WIDE = False


def mx_kscale(k):
    if not WIDE:
        return np.ones(k)
    levels = np.array([18, -18])
    if k % 512:
        return np.exp2(np.random.permutation(np.resize(levels, k // 32))).repeat(32)
    a = np.empty((k // 512, 16))
    for p in range(k // 512):
        a[p, :8] = np.random.permutation(np.resize(levels, 8))
        for g in range(8):
            far = levels[np.abs(levels - a[p, g]) >= 10]
            a[p, g + 8] = far[np.random.randint(len(far))]
    return np.exp2(a.ravel()).repeat(32)


def f64(x):
    return np.asarray(x).astype(np.float64)


def striped(idx):
    return np.tile(np.asarray(idx).reshape(-1, 16).T, (8, 1)).astype(np.uint16)


def unstriped(offs):
    return offs[:16].T.reshape(-1).astype(np.int64)


E2M1 = np.array([0.0, 0.5, 1.0, 1.5, 2.0, 3.0, 4.0, 6.0, -0.0, -0.5, -1.0, -1.5, -2.0, -3.0, -4.0, -6.0])


def pack_weight(w, fmt):
    k, n = w.shape
    w = f64(np.asarray(w, np.float32).astype(ml_dtypes.bfloat16)).reshape(k // 32, 32, n)
    amax = np.abs(w).max(1)
    if fmt == "e4m3":
        byte = np.frexp(amax)[1] - 1 + 127 - 7
    else:
        mant, ex = np.frexp(amax / 6.0)
        byte = np.where(mant > 0.5, ex, ex - 1) + 127
    byte = np.clip(np.where(amax > 0, byte, 1), 1, 254)
    scaled = (w * np.exp2(127.0 - byte)[:, None, :]).reshape(k, n).astype(np.float32)
    by_word = np.ascontiguousarray(scaled.reshape(k // 512, 128, 4, n).transpose(0, 1, 3, 2))
    if fmt == "e4m3":
        words = by_word.astype(ml_dtypes.float8_e4m3fn).view(np.uint8)
    else:
        c = by_word.astype(ml_dtypes.float4_e2m1fn).view(np.uint8) & 0xF
        words = (c[..., 0::2] | (c[..., 1::2] << 4)).reshape(k // 512, 128, 2 * n)
    return np.ascontiguousarray(words), np.ascontiguousarray(byte.astype(np.uint8).reshape(k // 512, 16, n))


def unpack_weight(words, scales, fmt):
    g, _, n = scales.shape
    words = np.ascontiguousarray(words).reshape(g, 128, n, -1)
    if fmt == "e4m3":
        vals = words.view(ml_dtypes.float8_e4m3fn).astype(np.float64)
    else:
        nib = np.empty((g, 128, n, 4), np.uint8)
        nib[..., 0::2] = words & 0xF
        nib[..., 1::2] = words >> 4
        vals = E2M1[nib]
    vals = vals * np.repeat(np.exp2(scales.astype(np.float64) - 127.0), 8, axis=1)[..., None]
    return vals.transpose(0, 1, 3, 2).reshape(g * 512, n)


B, N, T, D, R = 2, 512, 2048, 512, 512


def setup_inputs():
    n = np.random.standard_normal
    idx = np.random.permutation(T)[:B * N]
    s = mx_kscale(D)[:, None]
    z = mx_kscale(R)[:, None]
    x = n((B, D, R))
    vp = pack_weight(n((D, T)) * (0.50 / np.sqrt(D)) / s, "e4m3")
    return {
        "xT": (x * s).astype(np.float32),
        "wT": (n((D, T)) * (0.50 / np.sqrt(D)) / s).astype(np.float32),
        "v_words": vp[0],
        "v_scales": vp[1],
        "wt": (np.random.uniform(0.5, 1.5, (B, R, 1)) * N / np.sqrt(R) * z).astype(np.float32),
        "xm": (x.transpose(0, 2, 1) / z).astype(np.float32),
        "offs": striped(idx),
    }


def reference(xT, wT, v_words, v_scales, wt, xm, offs):
    idx = unstriped(offs)
    v = unpack_weight(v_words, v_scales, "e4m3")
    pick = lambda x: x[:, idx].reshape(x.shape[0], B, N).transpose(1, 0, 2)
    xq = mxq(f64(xT), 1, "e4m3").transpose(0, 2, 1)
    a = xq @ mxq(pick(f64(wT)), 1, "e4m3")
    av = xq @ pick(v)
    e = np.exp(a - a.max(-1, keepdims=True))
    f = np.exp(av - av.max(-1, keepdims=True))
    g = f64(wt) * (e / e.sum(-1, keepdims=True) - f / f.sum(-1, keepdims=True))
    dw = mxq(f64(xm), 1, "e4m3").transpose(0, 2, 1) @ mxq(g, 1, "e5m2")
    gw = np.zeros((D, T))
    gw[:, idx] = dw.transpose(1, 0, 2).reshape(D, B * N)
    return gw

@@ -1,0 +1,167 @@
+from contextlib import ExitStack
+
+import concourse.mybir as mybir
+
+B, N, T, D, R = 2, 512, 2048, 512, 512
+FLOPS = 3 * 2 * B * R * N * D
+
+F32 = mybir.dt.float32
+BF16 = mybir.dt.bfloat16
+I32 = mybir.dt.int32
+U32 = mybir.dt.uint32
+U16 = mybir.dt.uint16
+U8 = mybir.dt.uint8
+E4 = mybir.dt.float8_e4m3fn_x4
+E5 = mybir.dt.float8_e5m2_x4
+ALU = mybir.AluOpType
+ACT = mybir.ActivationFunctionType
+AX = mybir.AxisListType
+
+P = 128
+PACK = 4
+LC = N // 16
+
+
+def tile_attend_gds_kl_kernel(tc, xT, wT, v_words, v_scales, wt, xm, offs, out):
+    nc = tc.nc
+    with ExitStack() as ctx:
+        keep = ctx.enter_context(tc.tile_pool(name="keep", bufs=1))
+        ring = ctx.enter_context(tc.tile_pool(name="ring", bufs=2))
+        psum = ctx.enter_context(tc.psum_pool(name="psum", bufs=1))
+
+        def held(shape, dtype, name):
+            return keep.tile(shape, dtype, name=name, align_bytes=64)
+
+        offsets = keep.tile([P, B * LC], U16, name="offsets")
+        nc.sync.dma_start(offsets[:], offs)
+
+        def listed(b):
+            return offsets[:, b * LC:(b + 1) * LC]
+
+        warm = keep.tile([P, 1], F32, name="warm")
+        nc.gpsimd.memset(warm[:], 0.0)
+        warm2 = keep.tile([P, 1], F32, name="warm2")
+        nc.scalar.activation(warm2[:], warm[:], ACT.Exp)
+
+        vs_all = held([P, T], U8, "vs_all")
+        nc.gpsimd.memset(vs_all[:].bitcast(I32), 0)
+        for q in range(4):
+            nc.scalar.dma_start(vs_all[32 * q:32 * q + 4, :].bitcast(I32), v_scales[0, 4 * q:4 * q + 4, :].bitcast(I32))
+        wt_sb = held([P, B, PACK], F32, "wt_sb")
+        nc.scalar.dma_start(wt_sb[:], wt.rearrange("b (s t) o -> s b (t o)", t=PACK))
+
+        vw_all = held([P, T], I32, "vw_all")
+        nc.sync.dma_start(vw_all[:], v_words[0].rearrange("p n t -> p (n t)").bitcast(I32))
+        x_raw = [held([P, PACK, R], F32, f"x_raw{b}") for b in range(B)]
+        xm_raw = [held([P, PACK, D], F32, f"xm_raw{b}") for b in range(B)]
+        w_plane = [held([P, T], F32, f"w_plane{j}") for j in range(PACK)]
+        nc.sync.dma_start(x_raw[0][:], xT[0].rearrange("(p j) r -> p j r", j=PACK))
+        w_rows = wT.rearrange("(p j) t -> j p t", j=PACK)
+        for j in (2, 3, 0, 1):
+            nc.sync.dma_start(w_plane[j][:], w_rows[j])
+        nc.sync.dma_start(xm_raw[0][:], xm[0].rearrange("(p j) d -> p j d", j=PACK))
+        nc.sync.dma_start(x_raw[1][:], xT[1].rearrange("(p j) r -> p j r", j=PACK))
+        nc.sync.dma_start(xm_raw[1][:], xm[1].rearrange("(p j) d -> p j d", j=PACK))
+
+        window = [held([P, T], F32, f"window{m}") for m in range(D // P)]
+        for m in range(D // P):
+            (nc.vector if m < 1 else nc.gpsimd).memset(window[m][:].bitcast(I32), 0)
+
+        def quantise(grouped, fmt, name):
+            codes = held([P, N], U32, name + "_codes")
+            scales = held([P, N], U8, name + "_scales")
+            nc.vector.quantize_mx(out=codes[:].bitcast(fmt), scales=scales[:], in_=grouped[:])
+            return codes, scales
+
+        def gather_teacher(b):
+            scales = held([P, N], U8, f"v_scales{b}")
+            nc.vector.tensor_copy(scales[:], vs_all[:].indirect(listed(b)))
+            codes = held([P, N], U32, f"v_codes{b}")
+            nc.vector.tensor_copy(codes[:], vw_all[:].bitcast(U32).indirect(listed(b)))
+            return codes, scales
+
+        def group_x(b, copy):
+            grouped = held([P, PACK * R], BF16, f"xg{b}")
+            copy(grouped[:].rearrange("p (t s j) -> p s j t", t=PACK, j=PACK),
+                           x_raw[b][:].rearrange("p j (s t) -> p s j t", t=PACK))
+            return grouped
+
+        def group_rows(src, name, copy):
+            grouped = held([P, PACK * N], BF16, name)
+            copy(grouped[:].rearrange("p (c i j) -> p c j i", i=4, j=PACK),
+                           src.rearrange("p j (c i) -> p c j i", i=4))
+            return grouped
+
+        def softmax_side(xq, cols, b, name):
+            neg_max = held([P, PACK], F32, name + "_max")
+            total = held([P, PACK], F32, name + "_sum")
+            factor = held([P, PACK], F32, name + "_factor")
+            inv = held([P, PACK], F32, name + "_inv")
+            e = held([P, PACK, N], F32, name + "_e")
+            for t in range(PACK):
+                bank = psum.tile([P, N], F32, name="scores", tag="scores", bufs=6)
+                nc.tensor.matmul_mx(out=bank[:], lhsT=xq[0][:, t * P:(t + 1) * P].bitcast(E4),
+                                    lhsT_scale=xq[1][:, t * P:(t + 1) * P],
+                                    rhs=cols[0][:].bitcast(E4), rhs_scale=cols[1][:], start=True, stop=True)
+                nc.vector.tensor_reduce(neg_max[:, t:t + 1], bank[:], AX.X, ALU.max, negate=True)
+                nc.scalar.activation(e[:, t, :], bank[:], ACT.Exp, bias=neg_max[:, t:t + 1], accum_out=total[:, t:t + 1])
+            nc.vector.reciprocal(inv[:], total[:])
+            nc.vector.tensor_tensor(factor[:], inv[:], wt_sb[:, b, :], ALU.mult)
+            for t in range(PACK):
+                nc.scalar.activation(e[:, t, :], e[:, t, :], ACT.Copy, scale=factor[:, t:t + 1])
+            return e
+
+        def gradient(e, z, b):
+            g = held([P, PACK * N], BF16, f"g{b}")
+            nc.vector.tensor_tensor(g[:].rearrange("p (c i t) -> p c t i", i=4, t=PACK),
+                                    e[:].rearrange("p t (c i) -> p c t i", i=4),
+                                    z[:].rearrange("p t (c i) -> p c t i", i=4), ALU.subtract)
+            return quantise(g, E5, f"gq{b}")
+
+        def table_gradient(xmq, gq, b, m, stage_name):
+            bank = psum.tile([P, N], F32, name="dw", tag="dw", bufs=2)
+            nc.tensor.matmul_mx(out=bank[:], lhsT=xmq[0][:, m * P:(m + 1) * P].bitcast(E4),
+                                lhsT_scale=xmq[1][:, m * P:(m + 1) * P],
+                                rhs=gq[0][:].bitcast(E5), rhs_scale=gq[1][:], start=True, stop=True)
+            dw = held([P, N], F32, stage_name)
+            nc.scalar.copy(dw[:], bank[:])
+            nc.vector.tensor_copy(window[m][:].indirect(listed(b)), dw[:])
+            if b == B - 1:
+                nc.sync.dma_start(out[m * P:(m + 1) * P, :], window[m][:])
+
+        vcopy, scopy = nc.vector.tensor_copy, nc.scalar.copy
+        v0 = gather_teacher(0)
+        xq0 = quantise(group_x(0, vcopy), E4, "xq0")
+        v1 = gather_teacher(1)
+        z0 = softmax_side(xq0, v0, 0, "t0")
+        w_picked = held([P, PACK + 2, N], BF16, "w_picked")
+        w_cast = held([P, T], BF16, "w_cast")
+        nc.scalar.copy(w_cast[:], w_plane[2][:])
+
+        def pick(j, b):
+            dst = w_picked[:, 2 * b + j, :]
+            if j == 2:
+                nc.scalar.activation(dst, w_cast[:].indirect(listed(b)), ACT.Copy)
+            else:
+                nc.vector.tensor_copy(dst, w_plane[j][:].indirect(listed(b)))
+
+        for j in (2, 3, 0, 1):
+            pick(j, 0)
+        wq0 = quantise(group_rows(w_picked[:, 0:PACK, :], "wg0", vcopy), E4, "wq0")
+        e0 = softmax_side(xq0, wq0, 0, "s0")
+        xmq0 = quantise(group_rows(xm_raw[0][:], "xmg0", scopy), E4, "xmq0")
+        gq0 = gradient(e0, z0, 0)
+        table_gradient(xmq0, gq0, 0, 0, "dw00")
+        for j in (2, 3, 0, 1):
+            pick(j, 1)
+        xq1 = quantise(group_x(1, vcopy), E4, "xq1")
+        wq1 = quantise(group_rows(w_picked[:, 2:2 + PACK, :], "wg1", scopy), E4, "wq1")
+        z1 = softmax_side(xq1, v1, 1, "t1")
+        e1 = softmax_side(xq1, wq1, 1, "s1")
+        xmq1 = quantise(group_rows(xm_raw[1][:], "xmg1", scopy), E4, "xmq1")
+        table_gradient(xmq0, gq0, 0, 1, "dw01")
+        gq1 = gradient(e1, z1, 1)
+        table_gradient(xmq0, gq0, 0, 2, "s1_e")
+        table_gradient(xmq0, gq0, 0, 3, "g1")
+        for m in range(D // P):
+            table_gradient(xmq1, gq1, 1, m, f"dw1{m}")

@@ -11,157 +11,205 @@ I32 = mybir.dt.int32
 U32 = mybir.dt.uint32
 U16 = mybir.dt.uint16
 U8 = mybir.dt.uint8
-E4 = mybir.dt.float8_e4m3fn_x4
-E5 = mybir.dt.float8_e5m2_x4
+E4M3 = mybir.dt.float8_e4m3fn_x4
+E5M2 = mybir.dt.float8_e5m2_x4
 ALU = mybir.AluOpType
 ACT = mybir.ActivationFunctionType
-AX = mybir.AxisListType
+AXIS = mybir.AxisListType
 
 P = 128
 PACK = 4
-LC = N // 16
+RUN = 4
+LIST_COLUMNS = N // 16
+QUADRANT = 32
+HALVES = 2
+SCORE_BANKS, RESULT_BANKS = 6, 2
+SCALAR_PLANES = (2, 3)
+VECTOR_PLANES = (0, 1)
 
 
 def tile_attend_gds_kl_kernel(tc, xT, wT, v_words, v_scales, wt, xm, offs, out):
     nc = tc.nc
     with ExitStack() as ctx:
         keep = ctx.enter_context(tc.tile_pool(name="keep", bufs=1))
-        ring = ctx.enter_context(tc.tile_pool(name="ring", bufs=2))
         psum = ctx.enter_context(tc.psum_pool(name="psum", bufs=1))
 
-        def held(shape, dtype, name):
-            return keep.tile(shape, dtype, name=name, align_bytes=64)
+        def held(shape, dtype, name, after=None):
+            return keep.tile(shape, dtype, name=name, tag=after or name, align_bytes=64)
 
-        offsets = keep.tile([P, B * LC], U16, name="offsets")
+        offsets = keep.tile([P, B * LIST_COLUMNS], U16, name="offsets")
         nc.sync.dma_start(offsets[:], offs)
 
         def listed(b):
-            return offsets[:, b * LC:(b + 1) * LC]
+            return offsets[:, b * LIST_COLUMNS:(b + 1) * LIST_COLUMNS]
 
-        warm = keep.tile([P, 1], F32, name="warm")
-        nc.gpsimd.memset(warm[:], 0.0)
-        warm2 = keep.tile([P, 1], F32, name="warm2")
-        nc.scalar.activation(warm2[:], warm[:], ACT.Exp)
-
-        vs_all = held([P, T], U8, "vs_all")
-        nc.gpsimd.memset(vs_all[:].bitcast(I32), 0)
-        for q in range(4):
-            nc.scalar.dma_start(vs_all[32 * q:32 * q + 4, :].bitcast(I32), v_scales[0, 4 * q:4 * q + 4, :].bitcast(I32))
-        wt_sb = held([P, B, PACK], F32, "wt_sb")
-        nc.scalar.dma_start(wt_sb[:], wt.rearrange("b (s t) o -> s b (t o)", t=PACK))
-
-        vw_all = held([P, T], I32, "vw_all")
-        nc.sync.dma_start(vw_all[:], v_words[0].rearrange("p n t -> p (n t)").bitcast(I32))
+        v_scale_rows = held([P, T], U8, "v_scale_rows")
+        nc.gpsimd.memset(v_scale_rows[:].bitcast(I32), 0)
+        weight = held([P, B, PACK], F32, "weight")
+        v_word_rows = held([P, T], I32, "v_word_rows")
         x_raw = [held([P, PACK, R], F32, f"x_raw{b}") for b in range(B)]
         xm_raw = [held([P, PACK, D], F32, f"xm_raw{b}") for b in range(B)]
         w_plane = [held([P, T], F32, f"w_plane{j}") for j in range(PACK)]
-        nc.sync.dma_start(x_raw[0][:], xT[0].rearrange("(p j) r -> p j r", j=PACK))
         w_rows = wT.rearrange("(p j) t -> j p t", j=PACK)
-        for j in (2, 3, 0, 1):
-            nc.sync.dma_start(w_plane[j][:], w_rows[j])
-        nc.sync.dma_start(xm_raw[0][:], xm[0].rearrange("(p j) d -> p j d", j=PACK))
-        nc.sync.dma_start(x_raw[1][:], xT[1].rearrange("(p j) r -> p j r", j=PACK))
-        nc.sync.dma_start(xm_raw[1][:], xm[1].rearrange("(p j) d -> p j d", j=PACK))
 
-        window = [held([P, T], F32, f"window{m}") for m in range(D // P)]
-        for m in range(D // P):
-            (nc.vector if m < 1 else nc.gpsimd).memset(window[m][:].bitcast(I32), 0)
+        def load_plane(j):
+            nc.sync.dma_start(w_plane[j][:], w_rows[j])
+
+        def load_x(b):
+            nc.sync.dma_start(x_raw[b][:], xT[b].rearrange("(p j) r -> p j r", j=PACK))
+
+        def load_xm(b):
+            nc.sync.dma_start(xm_raw[b][:], xm[b].rearrange("(p j) d -> p j d", j=PACK))
+
+        nc.sync.dma_start(weight[:], wt.rearrange("b (s t) o -> s b (t o)", t=PACK))
+        for q in range(PACK):
+            nc.sync.dma_start(v_scale_rows[q:P:QUADRANT, :].bitcast(I32), v_scales[0, q:D // 32:PACK, :].bitcast(I32))
+        nc.sync.dma_start(v_word_rows[:], v_words[0].rearrange("p n t -> p (n t)").bitcast(I32))
+        load_plane(SCALAR_PLANES[0])
+        load_x(0)
+        load_plane(SCALAR_PLANES[1])
+        for j in VECTOR_PLANES:
+            load_plane(j)
+        load_xm(0)
+        load_x(1)
+        load_xm(1)
+
+        window = {}
+        for m in range(2):
+            window[m] = held([P, T], F32, f"window{m}")
+            nc.vector.memset(window[m][:].bitcast(I32), 0)
+
+        def late_window(m, after):
+            window[m] = held([P, T], F32, f"window{m}", after)
+            for c in range(0, T, N):
+                nc.gpsimd.memset(window[m][:, c:c + N].bitcast(I32), 0)
 
         def quantise(grouped, fmt, name):
             codes = held([P, N], U32, name + "_codes")
             scales = held([P, N], U8, name + "_scales")
-            nc.vector.quantize_mx(out=codes[:].bitcast(fmt), scales=scales[:], in_=grouped[:])
+            nc.vector.quantize_mx(out=codes[:].bitcast(fmt), scales=scales[:], in_=grouped)
             return codes, scales
+
+        def product(bank, stationary, block, moving, moving_fmt):
+            cols = slice(block * P, (block + 1) * P)
+            nc.tensor.matmul_mx(out=bank[:], lhsT=stationary[0][:, cols].bitcast(E4M3), lhsT_scale=stationary[1][:, cols],
+                                rhs=moving[0][:].bitcast(moving_fmt), rhs_scale=moving[1][:], start=True, stop=True)
 
         def gather_teacher(b):
             scales = held([P, N], U8, f"v_scales{b}")
-            nc.vector.tensor_copy(scales[:], vs_all[:].indirect(listed(b)))
+            nc.vector.tensor_copy(scales[:], v_scale_rows[:].indirect(listed(b)))
             codes = held([P, N], U32, f"v_codes{b}")
-            nc.vector.tensor_copy(codes[:], vw_all[:].bitcast(U32).indirect(listed(b)))
+            nc.vector.tensor_copy(codes[:], v_word_rows[:].bitcast(U32).indirect(listed(b)))
             return codes, scales
 
-        def group_x(b, copy):
-            grouped = held([P, PACK * R], BF16, f"xg{b}")
-            copy(grouped[:].rearrange("p (t s j) -> p s j t", t=PACK, j=PACK),
-                           x_raw[b][:].rearrange("p j (s t) -> p s j t", t=PACK))
-            return grouped
+        picked_places = held([P, PACK + 2, N], BF16, "picked")
+        picked = [picked_places[:, 2 * b:2 * b + PACK, :] for b in range(B)]
+        w_cast = {}
 
-        def group_rows(src, name, copy):
-            grouped = held([P, PACK * N], BF16, name)
-            copy(grouped[:].rearrange("p (c i j) -> p c j i", i=4, j=PACK),
-                           src.rearrange("p j (c i) -> p c j i", i=4))
-            return grouped
-
-        def softmax_side(xq, cols, b, name):
-            neg_max = held([P, PACK], F32, name + "_max")
-            total = held([P, PACK], F32, name + "_sum")
-            factor = held([P, PACK], F32, name + "_factor")
-            inv = held([P, PACK], F32, name + "_inv")
-            e = held([P, PACK, N], F32, name + "_e")
-            for t in range(PACK):
-                bank = psum.tile([P, N], F32, name="scores", tag="scores", bufs=6)
-                nc.tensor.matmul_mx(out=bank[:], lhsT=xq[0][:, t * P:(t + 1) * P].bitcast(E4),
-                                    lhsT_scale=xq[1][:, t * P:(t + 1) * P],
-                                    rhs=cols[0][:].bitcast(E4), rhs_scale=cols[1][:], start=True, stop=True)
-                nc.vector.tensor_reduce(neg_max[:, t:t + 1], bank[:], AX.X, ALU.max, negate=True)
-                nc.scalar.activation(e[:, t, :], bank[:], ACT.Exp, bias=neg_max[:, t:t + 1], accum_out=total[:, t:t + 1])
-            nc.vector.reciprocal(inv[:], total[:])
-            nc.vector.tensor_tensor(factor[:], inv[:], wt_sb[:, b, :], ALU.mult)
-            for t in range(PACK):
-                nc.scalar.activation(e[:, t, :], e[:, t, :], ACT.Copy, scale=factor[:, t:t + 1])
-            return e
-
-        def gradient(e, z, b):
-            g = held([P, PACK * N], BF16, f"g{b}")
-            nc.vector.tensor_tensor(g[:].rearrange("p (c i t) -> p c t i", i=4, t=PACK),
-                                    e[:].rearrange("p t (c i) -> p c t i", i=4),
-                                    z[:].rearrange("p t (c i) -> p c t i", i=4), ALU.subtract)
-            return quantise(g, E5, f"gq{b}")
-
-        def table_gradient(xmq, gq, b, m, stage_name):
-            bank = psum.tile([P, N], F32, name="dw", tag="dw", bufs=2)
-            nc.tensor.matmul_mx(out=bank[:], lhsT=xmq[0][:, m * P:(m + 1) * P].bitcast(E4),
-                                lhsT_scale=xmq[1][:, m * P:(m + 1) * P],
-                                rhs=gq[0][:].bitcast(E5), rhs_scale=gq[1][:], start=True, stop=True)
-            dw = held([P, N], F32, stage_name)
-            nc.scalar.copy(dw[:], bank[:])
-            nc.vector.tensor_copy(window[m][:].indirect(listed(b)), dw[:])
-            if b == B - 1:
-                nc.sync.dma_start(out[m * P:(m + 1) * P, :], window[m][:])
-
-        vcopy, scopy = nc.vector.tensor_copy, nc.scalar.copy
-        v0 = gather_teacher(0)
-        xq0 = quantise(group_x(0, vcopy), E4, "xq0")
-        v1 = gather_teacher(1)
-        z0 = softmax_side(xq0, v0, 0, "t0")
-        w_picked = held([P, PACK + 2, N], BF16, "w_picked")
-        w_cast = held([P, T], BF16, "w_cast")
-        nc.scalar.copy(w_cast[:], w_plane[2][:])
+        def cast_plane(j):
+            w_cast[j] = held([P, T], BF16, f"w_cast{j}")
+            nc.scalar.activation(w_cast[j][:], w_plane[j][:], ACT.Copy)
 
         def pick(j, b):
-            dst = w_picked[:, 2 * b + j, :]
-            if j == 2:
-                nc.scalar.activation(dst, w_cast[:].indirect(listed(b)), ACT.Copy)
+            if j in SCALAR_PLANES:
+                nc.scalar.activation(picked[b][:, j, :], w_cast[j][:].indirect(listed(b)), ACT.Copy)
             else:
-                nc.vector.tensor_copy(dst, w_plane[j][:].indirect(listed(b)))
+                nc.vector.tensor_copy(picked[b][:, j, :], w_plane[j][:].indirect(listed(b)))
 
-        for j in (2, 3, 0, 1):
+        def group_dealt(b, copy):
+            grouped = held([P, PACK * R], BF16, f"x_grouped{b}")
+            copy(grouped[:].rearrange("p (t s j) -> p s j t", t=PACK, j=PACK),
+                 x_raw[b][:].rearrange("p j (s t) -> p s j t", t=PACK))
+            return grouped[:]
+
+        def group_plain(rows, name, copy, after=None):
+            grouped = held([P, PACK * N], BF16, name, after)
+            copy(grouped[:].rearrange("p (c i j) -> p c j i", i=RUN, j=PACK), rows.rearrange("p j (c i) -> p c j i", i=RUN))
+            return grouped[:]
+
+        def exponentials(xq, table, name, total, parts):
+            neg_max = held([P, PACK], F32, name + "_max")
+            e = held([P, parts, PACK, N // parts], F32, name + "_e")
+            for t in range(PACK):
+                bank = psum.tile([P, N], F32, name="scores", tag="scores", bufs=SCORE_BANKS)
+                product(bank, xq, t, table, E4M3)
+                nc.vector.tensor_reduce(neg_max[:, t:t + 1], bank[:], AXIS.X, ALU.max, negate=True)
+                nc.scalar.activation(e[:, :, t, :], bank[:].rearrange("p (h c) -> p h c", h=parts), ACT.Exp,
+                                     bias=neg_max[:, t:t + 1], accum_out=total[:, t:t + 1])
+            return e
+
+        def scatter_block(xmq, gq, b, m, after=None):
+            bank = psum.tile([P, N], F32, name="result", tag="result", bufs=RESULT_BANKS)
+            product(bank, xmq, m, gq, E5M2)
+            staged = held([P, N], F32, f"staged{b}{m}", after)
+            nc.scalar.copy(staged[:], bank[:])
+            nc.vector.tensor_copy(window[m][:].indirect(listed(b)), staged[:])
+
+        v0 = gather_teacher(0)
+        xq0 = quantise(group_dealt(0, nc.vector.tensor_copy), E4M3, "xq0")
+        v1 = gather_teacher(1)
+        teacher_sum0 = held([P, PACK], F32, "teacher_sum0")
+        teacher_inv0 = held([P, PACK], F32, "teacher_inv0")
+        z0 = exponentials(xq0, v0, "teacher0", teacher_sum0, 1)[:, 0, :, :]
+        nc.vector.reciprocal(teacher_inv0[:], teacher_sum0[:])
+        teacher_factor0 = held([P, PACK], F32, "teacher_factor0")
+        nc.vector.tensor_tensor(teacher_factor0[:], teacher_inv0[:], weight[:, 0, :], ALU.mult)
+        for t in range(PACK):
+            nc.scalar.activation(z0[:, t, :], z0[:, t, :], ACT.Copy, scale=teacher_factor0[:, t:t + 1])
+
+        for j in SCALAR_PLANES:
+            cast_plane(j)
             pick(j, 0)
-        wq0 = quantise(group_rows(w_picked[:, 0:PACK, :], "wg0", vcopy), E4, "wq0")
-        e0 = softmax_side(xq0, wq0, 0, "s0")
-        xmq0 = quantise(group_rows(xm_raw[0][:], "xmg0", scopy), E4, "xmq0")
-        gq0 = gradient(e0, z0, 0)
-        table_gradient(xmq0, gq0, 0, 0, "dw00")
-        for j in (2, 3, 0, 1):
+        for j in VECTOR_PLANES:
+            pick(j, 0)
+        w_grouped0 = group_plain(picked[0], "w_grouped0", nc.vector.tensor_copy)
+        pick(VECTOR_PLANES[0], 1)
+        wq0 = quantise(w_grouped0, E4M3, "wq0")
+        student_sum0 = held([P, PACK], F32, "student_sum0")
+        student_inv0 = held([P, PACK], F32, "student_inv0")
+        e0 = exponentials(xq0, wq0, "student0", student_sum0, 1)[:, 0, :, :]
+        nc.vector.reciprocal(student_inv0[:], student_sum0[:])
+        for t in range(PACK):
+            nc.vector.tensor_scalar(e0[:, t, :], e0[:, t, :], student_inv0[:, t:t + 1], weight[:, 0, t:t + 1], ALU.mult, ALU.mult)
+        xmq0 = quantise(group_plain(xm_raw[0][:], "xm_grouped0", nc.scalar.copy), E4M3, "xmq0")
+
+        g0 = held([P, PACK * N], BF16, "g0")
+        nc.vector.tensor_tensor(g0[:].rearrange("p (c i t) -> p c t i", i=RUN, t=PACK),
+                                e0.rearrange("p t (c i) -> p c t i", i=RUN),
+                                z0.rearrange("p t (c i) -> p c t i", i=RUN), ALU.subtract)
+        gq0 = quantise(g0[:], E5M2, "gq0")
+
+        for j in SCALAR_PLANES + VECTOR_PLANES[1:]:
             pick(j, 1)
-        xq1 = quantise(group_x(1, vcopy), E4, "xq1")
-        wq1 = quantise(group_rows(w_picked[:, 2:2 + PACK, :], "wg1", scopy), E4, "wq1")
-        z1 = softmax_side(xq1, v1, 1, "t1")
-        e1 = softmax_side(xq1, wq1, 1, "s1")
-        xmq1 = quantise(group_rows(xm_raw[1][:], "xmg1", scopy), E4, "xmq1")
-        table_gradient(xmq0, gq0, 0, 1, "dw01")
-        gq1 = gradient(e1, z1, 1)
-        table_gradient(xmq0, gq0, 0, 2, "s1_e")
-        table_gradient(xmq0, gq0, 0, 3, "g1")
-        for m in range(D // P):
-            table_gradient(xmq1, gq1, 1, m, f"dw1{m}")
+        xq1 = quantise(group_dealt(1, nc.scalar.copy), E4M3, "xq1")
+        wq1 = quantise(group_plain(picked[1], "w_grouped1", nc.scalar.copy), E4M3, "wq1")
+        sums1 = held([P, 2, PACK], F32, "sums1")
+        z1 = exponentials(xq1, v1, "teacher1", sums1[:, 0, :], HALVES)
+        e1 = exponentials(xq1, wq1, "student1", sums1[:, 1, :], HALVES)
+
+        scatter_block(xmq0, gq0, 0, 0, after="student1_max")
+        inv1 = held([P, 2, PACK], F32, "inv1")
+        factor1 = held([P, 2, PACK], F32, "factor1")
+        nc.vector.reciprocal(inv1[:], sums1[:])
+        nc.vector.tensor_tensor(factor1[:], inv1[:], weight[:, 1:2, :].to_broadcast([P, 2, PACK]), ALU.mult)
+        for part in range(HALVES):
+            for side, values in enumerate((z1, e1)):
+                for t in range(PACK):
+                    nc.scalar.activation(values[:, part, t, :], values[:, part, t, :], ACT.Copy, scale=factor1[:, side, t:t + 1])
+        scatter_block(xmq0, gq0, 0, 1)
+        late_window(2, after="g0")
+        scatter_block(xmq0, gq0, 0, 2)
+        xmq1 = quantise(group_plain(xm_raw[1][:], "xm_grouped1", nc.scalar.copy, after="xm_grouped0"), E4M3, "xmq1")
+
+        g1 = held([P, HALVES, N // HALVES, PACK], BF16, "g1")
+        for part in range(HALVES):
+            nc.gpsimd.tensor_tensor(g1[:, part, :, :], e1[:, part, :, :].rearrange("p t c -> p c t"),
+                                    z1[:, part, :, :].rearrange("p t c -> p c t"), ALU.subtract)
+        gq1 = quantise(g1[:].rearrange("p h c t -> p (h c t)"), E5M2, "gq1")
+
+        late_window(3, after="xq1_codes")
+        scatter_block(xmq0, gq0, 0, 3, after="student1_e")
+
+        for m, free in enumerate(("xm_raw0", "w_plane0", "x_raw0", "w_plane1")):
+            scatter_block(xmq1, gq1, 1, m, after=free)
+            nc.sync.dma_start(out[m * P:(m + 1) * P, :], window[m][:])

@@ -75,14 +75,9 @@ def tile_attend_gds_kl_kernel(tc, xT, wT, v_words, v_scales, wt, xm, offs, out):
         load_xm(1)
 
         window = {}
-        for m in range(2):
+        for m in range(D // P - 1):
             window[m] = held([P, T], F32, f"window{m}")
             nc.vector.memset(window[m][:].bitcast(I32), 0)
-
-        def late_window(m, after):
-            window[m] = held([P, T], F32, f"window{m}", after)
-            for c in range(0, T, N):
-                nc.gpsimd.memset(window[m][:, c:c + N].bitcast(I32), 0)
 
         def quantise(grouped, fmt, name):
             codes = held([P, N], U32, name + "_codes")
@@ -177,11 +172,11 @@ def tile_attend_gds_kl_kernel(tc, xT, wT, v_words, v_scales, wt, xm, offs, out):
         nc.vector.tensor_tensor(g0[:].rearrange("p (c i t) -> p c t i", i=RUN, t=PACK),
                                 e0.rearrange("p t (c i) -> p c t i", i=RUN),
                                 z0.rearrange("p t (c i) -> p c t i", i=RUN), ALU.subtract)
-        gq0 = quantise(g0[:], E5M2, "gq0")
 
         for j in SCALAR_PLANES + VECTOR_PLANES[1:]:
             pick(j, 1)
         xq1 = quantise(group_dealt(1, nc.scalar.copy), E4M3, "xq1")
+        gq0 = quantise(g0[:], E5M2, "gq0")
         wq1 = quantise(group_plain(picked[1], "w_grouped1", nc.scalar.copy), E4M3, "wq1")
         sums1 = held([P, 2, PACK], F32, "sums1")
         z1 = exponentials(xq1, v1, "teacher1", sums1[:, 0, :], HALVES)
@@ -192,12 +187,14 @@ def tile_attend_gds_kl_kernel(tc, xT, wT, v_words, v_scales, wt, xm, offs, out):
         factor1 = held([P, 2, PACK], F32, "factor1")
         nc.vector.reciprocal(inv1[:], sums1[:])
         nc.vector.tensor_tensor(factor1[:], inv1[:], weight[:, 1:2, :].to_broadcast([P, 2, PACK]), ALU.mult)
+        last = D // P - 1
+        window[last] = held([P, T], F32, f"window{last}", after="inv1")
+        nc.gpsimd.memset(window[last][:].bitcast(I32), 0)
         for part in range(HALVES):
             for side, values in enumerate((z1, e1)):
                 for t in range(PACK):
                     nc.scalar.activation(values[:, part, t, :], values[:, part, t, :], ACT.Copy, scale=factor1[:, side, t:t + 1])
         scatter_block(xmq0, gq0, 0, 1)
-        late_window(2, after="g0")
         scatter_block(xmq0, gq0, 0, 2)
         xmq1 = quantise(group_plain(xm_raw[1][:], "xm_grouped1", nc.scalar.copy, after="xm_grouped0"), E4M3, "xmq1")
 
@@ -207,7 +204,6 @@ def tile_attend_gds_kl_kernel(tc, xT, wT, v_words, v_scales, wt, xm, offs, out):
                                     z1[:, part, :, :].rearrange("p t c -> p c t"), ALU.subtract)
         gq1 = quantise(g1[:].rearrange("p h c t -> p (h c t)"), E5M2, "gq1")
 
-        late_window(3, after="xq1_codes")
         scatter_block(xmq0, gq0, 0, 3, after="student1_e")
 
         for m, free in enumerate(("xm_raw0", "w_plane0", "x_raw0", "w_plane1")):

from contextlib import ExitStack

import concourse.mybir as mybir

B, N, T, D, R = 2, 512, 2048, 512, 512
FLOPS = 3 * 2 * B * R * N * D

F32 = mybir.dt.float32
BF16 = mybir.dt.bfloat16
I32 = mybir.dt.int32
U32 = mybir.dt.uint32
U16 = mybir.dt.uint16
U8 = mybir.dt.uint8
E4M3 = mybir.dt.float8_e4m3fn_x4
E5M2 = mybir.dt.float8_e5m2_x4
ALU = mybir.AluOpType
ACT = mybir.ActivationFunctionType
AXIS = mybir.AxisListType

P = 128
PACK = 4
RUN = 4
LIST_COLUMNS = N // 16
QUADRANT = 32
HALVES = 2
SCORE_BANKS, RESULT_BANKS = 6, 2
SCALAR_PLANES = (2, 3)
VECTOR_PLANES = (0, 1)


def tile_attend_gds_kl_kernel(tc, xT, wT, v_words, v_scales, wt, xm, offs, out):
    nc = tc.nc
    with ExitStack() as ctx:
        keep = ctx.enter_context(tc.tile_pool(name="keep", bufs=1))
        psum = ctx.enter_context(tc.psum_pool(name="psum", bufs=1))

        def held(shape, dtype, name, after=None):
            return keep.tile(shape, dtype, name=name, tag=after or name, align_bytes=64)

        offsets = keep.tile([P, B * LIST_COLUMNS], U16, name="offsets")
        nc.sync.dma_start(offsets[:], offs)

        def listed(b):
            return offsets[:, b * LIST_COLUMNS:(b + 1) * LIST_COLUMNS]

        v_scale_rows = held([P, T], U8, "v_scale_rows")
        nc.gpsimd.memset(v_scale_rows[:].bitcast(I32), 0)
        weight = held([P, B, PACK], F32, "weight")
        v_word_rows = held([P, T], I32, "v_word_rows")
        x_raw = [held([P, PACK, R], F32, f"x_raw{b}") for b in range(B)]
        xm_raw = [held([P, PACK, D], F32, f"xm_raw{b}") for b in range(B)]
        w_plane = [held([P, T], F32, f"w_plane{j}") for j in range(PACK)]
        w_rows = wT.rearrange("(p j) t -> j p t", j=PACK)

        def load_plane(j):
            nc.sync.dma_start(w_plane[j][:], w_rows[j])

        def load_x(b):
            nc.sync.dma_start(x_raw[b][:], xT[b].rearrange("(p j) r -> p j r", j=PACK))

        def load_xm(b):
            nc.sync.dma_start(xm_raw[b][:], xm[b].rearrange("(p j) d -> p j d", j=PACK))

        nc.sync.dma_start(weight[:], wt.rearrange("b (s t) o -> s b (t o)", t=PACK))
        for q in range(PACK):
            nc.sync.dma_start(v_scale_rows[q:P:QUADRANT, :].bitcast(I32), v_scales[0, q:D // 32:PACK, :].bitcast(I32))
        nc.sync.dma_start(v_word_rows[:], v_words[0].rearrange("p n t -> p (n t)").bitcast(I32))
        load_plane(SCALAR_PLANES[0])
        load_x(0)
        load_plane(SCALAR_PLANES[1])
        for j in VECTOR_PLANES:
            load_plane(j)
        load_xm(0)
        load_x(1)
        load_xm(1)

        window = {}
        for m in range(D // P - 1):
            window[m] = held([P, T], F32, f"window{m}")
            nc.vector.memset(window[m][:].bitcast(I32), 0)

        def quantise(grouped, fmt, name):
            codes = held([P, N], U32, name + "_codes")
            scales = held([P, N], U8, name + "_scales")
            nc.vector.quantize_mx(out=codes[:].bitcast(fmt), scales=scales[:], in_=grouped)
            return codes, scales

        def product(bank, stationary, block, moving, moving_fmt):
            cols = slice(block * P, (block + 1) * P)
            nc.tensor.matmul_mx(out=bank[:], lhsT=stationary[0][:, cols].bitcast(E4M3), lhsT_scale=stationary[1][:, cols],
                                rhs=moving[0][:].bitcast(moving_fmt), rhs_scale=moving[1][:], start=True, stop=True)

        def gather_teacher(b):
            scales = held([P, N], U8, f"v_scales{b}")
            nc.vector.tensor_copy(scales[:], v_scale_rows[:].indirect(listed(b)))
            codes = held([P, N], U32, f"v_codes{b}")
            nc.vector.tensor_copy(codes[:], v_word_rows[:].bitcast(U32).indirect(listed(b)))
            return codes, scales

        picked_places = held([P, PACK + 2, N], BF16, "picked")
        picked = [picked_places[:, 2 * b:2 * b + PACK, :] for b in range(B)]
        w_cast = {}

        def cast_plane(j):
            w_cast[j] = held([P, T], BF16, f"w_cast{j}")
            nc.scalar.activation(w_cast[j][:], w_plane[j][:], ACT.Copy)

        def pick(j, b):
            if j in SCALAR_PLANES:
                nc.scalar.activation(picked[b][:, j, :], w_cast[j][:].indirect(listed(b)), ACT.Copy)
            else:
                nc.vector.tensor_copy(picked[b][:, j, :], w_plane[j][:].indirect(listed(b)))

        def group_dealt(b, copy):
            grouped = held([P, PACK * R], BF16, f"x_grouped{b}")
            copy(grouped[:].rearrange("p (t s j) -> p s j t", t=PACK, j=PACK),
                 x_raw[b][:].rearrange("p j (s t) -> p s j t", t=PACK))
            return grouped[:]

        def group_plain(rows, name, copy, after=None):
            grouped = held([P, PACK * N], BF16, name, after)
            copy(grouped[:].rearrange("p (c i j) -> p c j i", i=RUN, j=PACK), rows.rearrange("p j (c i) -> p c j i", i=RUN))
            return grouped[:]

        def exponentials(xq, table, name, total, parts):
            neg_max = held([P, PACK], F32, name + "_max")
            e = held([P, parts, PACK, N // parts], F32, name + "_e")
            for t in range(PACK):
                bank = psum.tile([P, N], F32, name="scores", tag="scores", bufs=SCORE_BANKS)
                product(bank, xq, t, table, E4M3)
                nc.vector.tensor_reduce(neg_max[:, t:t + 1], bank[:], AXIS.X, ALU.max, negate=True)
                nc.scalar.activation(e[:, :, t, :], bank[:].rearrange("p (h c) -> p h c", h=parts), ACT.Exp,
                                     bias=neg_max[:, t:t + 1], accum_out=total[:, t:t + 1])
            return e

        def scatter_block(xmq, gq, b, m, after=None):
            bank = psum.tile([P, N], F32, name="result", tag="result", bufs=RESULT_BANKS)
            product(bank, xmq, m, gq, E5M2)
            staged = held([P, N], F32, f"staged{b}{m}", after)
            nc.scalar.copy(staged[:], bank[:])
            nc.vector.tensor_copy(window[m][:].indirect(listed(b)), staged[:])

        v0 = gather_teacher(0)
        xq0 = quantise(group_dealt(0, nc.vector.tensor_copy), E4M3, "xq0")
        v1 = gather_teacher(1)
        teacher_sum0 = held([P, PACK], F32, "teacher_sum0")
        teacher_inv0 = held([P, PACK], F32, "teacher_inv0")
        z0 = exponentials(xq0, v0, "teacher0", teacher_sum0, 1)[:, 0, :, :]
        nc.vector.reciprocal(teacher_inv0[:], teacher_sum0[:])
        teacher_factor0 = held([P, PACK], F32, "teacher_factor0")
        nc.vector.tensor_tensor(teacher_factor0[:], teacher_inv0[:], weight[:, 0, :], ALU.mult)
        for t in range(PACK):
            nc.scalar.activation(z0[:, t, :], z0[:, t, :], ACT.Copy, scale=teacher_factor0[:, t:t + 1])

        for j in SCALAR_PLANES:
            cast_plane(j)
            pick(j, 0)
        for j in VECTOR_PLANES:
            pick(j, 0)
        w_grouped0 = group_plain(picked[0], "w_grouped0", nc.vector.tensor_copy)
        pick(VECTOR_PLANES[0], 1)
        wq0 = quantise(w_grouped0, E4M3, "wq0")
        student_sum0 = held([P, PACK], F32, "student_sum0")
        student_inv0 = held([P, PACK], F32, "student_inv0")
        e0 = exponentials(xq0, wq0, "student0", student_sum0, 1)[:, 0, :, :]
        nc.vector.reciprocal(student_inv0[:], student_sum0[:])
        for t in range(PACK):
            nc.vector.tensor_scalar(e0[:, t, :], e0[:, t, :], student_inv0[:, t:t + 1], weight[:, 0, t:t + 1], ALU.mult, ALU.mult)
        xmq0 = quantise(group_plain(xm_raw[0][:], "xm_grouped0", nc.scalar.copy), E4M3, "xmq0")

        g0 = held([P, PACK * N], BF16, "g0")
        nc.vector.tensor_tensor(g0[:].rearrange("p (c i t) -> p c t i", i=RUN, t=PACK),
                                e0.rearrange("p t (c i) -> p c t i", i=RUN),
                                z0.rearrange("p t (c i) -> p c t i", i=RUN), ALU.subtract)

        for j in SCALAR_PLANES + VECTOR_PLANES[1:]:
            pick(j, 1)
        xq1 = quantise(group_dealt(1, nc.scalar.copy), E4M3, "xq1")
        gq0 = quantise(g0[:], E5M2, "gq0")
        wq1 = quantise(group_plain(picked[1], "w_grouped1", nc.scalar.copy), E4M3, "wq1")
        sums1 = held([P, 2, PACK], F32, "sums1")
        z1 = exponentials(xq1, v1, "teacher1", sums1[:, 0, :], HALVES)
        e1 = exponentials(xq1, wq1, "student1", sums1[:, 1, :], HALVES)

        scatter_block(xmq0, gq0, 0, 0, after="student1_max")
        inv1 = held([P, 2, PACK], F32, "inv1")
        factor1 = held([P, 2, PACK], F32, "factor1")
        nc.vector.reciprocal(inv1[:], sums1[:])
        nc.vector.tensor_tensor(factor1[:], inv1[:], weight[:, 1:2, :].to_broadcast([P, 2, PACK]), ALU.mult)
        last = D // P - 1
        window[last] = held([P, T], F32, f"window{last}", after="inv1")
        nc.gpsimd.memset(window[last][:].bitcast(I32), 0)
        for part in range(HALVES):
            for side, values in enumerate((z1, e1)):
                for t in range(PACK):
                    nc.scalar.activation(values[:, part, t, :], values[:, part, t, :], ACT.Copy, scale=factor1[:, side, t:t + 1])
        scatter_block(xmq0, gq0, 0, 1)
        scatter_block(xmq0, gq0, 0, 2)
        xmq1 = quantise(group_plain(xm_raw[1][:], "xm_grouped1", nc.scalar.copy, after="xm_grouped0"), E4M3, "xmq1")

        g1 = held([P, HALVES, N // HALVES, PACK], BF16, "g1")
        for part in range(HALVES):
            nc.gpsimd.tensor_tensor(g1[:, part, :, :], e1[:, part, :, :].rearrange("p t c -> p c t"),
                                    z1[:, part, :, :].rearrange("p t c -> p c t"), ALU.subtract)
        gq1 = quantise(g1[:].rearrange("p h c t -> p (h c t)"), E5M2, "gq1")

        scatter_block(xmq0, gq0, 0, 3, after="student1_e")

        for m, free in enumerate(("xm_raw0", "w_plane0", "x_raw0", "w_plane1")):
            scatter_block(xmq1, gq1, 1, m, after=free)
            nc.sync.dma_start(out[m * P:(m + 1) * P, :], window[m][:])
